import numpy as np
import ml_dtypes


def mxq(x, axis, fmt="e4m3"):
    dtype, down = {"e4m3": (ml_dtypes.float8_e4m3fn, 7), "e5m2": (ml_dtypes.float8_e5m2, 14)}[fmt]
    v = np.moveaxis(np.asarray(x, np.float32).astype(ml_dtypes.bfloat16).astype(np.float64), axis, -1)
    blocks = v.reshape(v.shape[:-1] + (-1, 32))
    amax = np.abs(blocks).max(-1, keepdims=True)
    byte = np.maximum(np.where(amax > 0, np.frexp(amax)[1] - 1 + 127, 0) - down, 1)
    scale = np.exp2(byte - 127.0)
    codes = (blocks / scale).astype(np.float32).astype(dtype).astype(np.float64)
    return np.moveaxis((codes * scale).reshape(v.shape), -1, axis)


WIDE = False


def mx_kscale(k):
    if not WIDE:
        return np.ones(k)
    levels = np.array([10, -10, 5, -5, 0])
    if k % 512:
        return np.exp2(np.random.permutation(np.resize(levels, k // 32))).repeat(32)
    a = np.empty((k // 512, 16))
    for p in range(k // 512):
        a[p, :8] = np.random.permutation(np.resize(levels, 8))
        for g in range(8):
            far = levels[np.abs(levels - a[p, g]) >= 10]
            a[p, g + 8] = far[np.random.randint(len(far))]
    return np.exp2(a.ravel()).repeat(32)


def f64(x):
    return np.asarray(x).astype(np.float64)


def striped(idx):
    return np.tile(idx.reshape(-1, 16).T, (8, 1)).astype(np.uint16)


def unstriped(offs):
    return offs[:16].T.reshape(-1).astype(np.int64)


def relu(v):
    return np.maximum(v, 0.0)


K, T, D, S, V, H, N = 512, 2048, 4, 768, 384, 512, 256


def setup_inputs():
    n = np.random.standard_normal
    s = mx_kscale(K)[:, None]
    u = mx_kscale(H)
    return {
        "xT": (n((K, T)) * s).astype(np.float32),
        "w1": (n((K, H)) / np.sqrt(K) / s * u).astype(np.float32),
        "w2": (n((H, N)) / np.sqrt(H) / u[:, None]).astype(np.float32),
        "gate": np.tile(np.random.uniform(0.2, 1.0, (D, 1, V)) / np.sqrt(D), (1, N, 1)).astype(np.float32),
        "offs": striped(np.random.permutation(T)[:S]),
        "pos1": striped(np.random.permutation(S)[:V]),
        "pos2": striped(np.random.permutation(S)[:V]),
        "pos3": striped(np.random.permutation(S)[:V]),
        "pos4": striped(np.random.permutation(S)[:V]),
    }


def reference(xT, w1, w2, gate, offs, pos1, pos2, pos3, pos4):
    idx = unstriped(offs)
    xq = mxq(f64(xT)[:, idx], 0, "e4m3")
    h = relu(mxq(f64(w1), 0, "e4m3").T @ xq)
    y = mxq(f64(w2), 0, "e4m3").T @ mxq(h, 0, "e4m3")
    return sum(f64(gate[d]) * y[:, unstriped(p)] for d, p in enumerate((pos1, pos2, pos3, pos4)))

@@ -1,0 +1,180 @@
+from contextlib import ExitStack
+
+import concourse.mybir as mybir
+
+K, T, D, S, V, H, N = 512, 2048, 4, 768, 384, 512, 256
+FLOPS = 2 * S * (K * H + H * N)
+
+F32 = mybir.dt.float32
+BF16 = mybir.dt.bfloat16
+U32 = mybir.dt.uint32
+U16 = mybir.dt.uint16
+U8 = mybir.dt.uint8
+FP8X4 = mybir.dt.float8_e4m3fn_x4
+ADD, MULT = mybir.AluOpType.add, mybir.AluOpType.mult
+RELU = mybir.ActivationFunctionType.Relu
+
+P = 128
+PACK = 4
+SLICE = 256
+SLICES = S // SLICE
+LANE = 16
+
+
+def tile_picked_sub_mlp_relu_sub_e_kernel(tc, xT, w1, w2, gate, offs, pos1, pos2, pos3, pos4, out):
+    nc = tc.nc
+    with ExitStack() as ctx:
+        keep = ctx.enter_context(tc.tile_pool(name="keep", bufs=1))
+        psum = ctx.enter_context(tc.psum_pool(name="psum", bufs=1))
+
+        def sb(shape, dtype, name):
+            return keep.tile(shape, dtype, name=name, align_bytes=64)
+
+        offs_sb = keep.tile([P, S // LANE], U16, name="offs_sb")
+        pos_sb = [keep.tile([P, V // LANE], U16, name=f"pos_sb{d}") for d in range(D)]
+
+        x_raw = [sb([P, T], F32, f"x_raw{j}") for j in range(PACK)]
+        w1_raw = sb([P, PACK, H], F32, "w1_raw")
+        w2_raw = sb([P, PACK, N], F32, "w2_raw")
+        gates = [sb([P, N // P, V], F32, f"gate{d}") for d in range(D)]
+
+        xv = xT.rearrange("(p j) t -> p j t", j=PACK)
+        nc.sync.dma_start(offs_sb[:], offs)
+        for j in range(3):
+            nc.sync.dma_start(out=x_raw[j][:], in_=xv[:, j, :])
+        nc.sync.dma_start(out=w1_raw[:], in_=w1.rearrange("(p j) c -> p j c", j=PACK))
+        nc.sync.dma_start(out=x_raw[3][:], in_=xv[:, 3, :])
+        nc.sync.dma_start(out=w2_raw[:], in_=w2.rearrange("(p j) c -> p j c", j=PACK))
+        for d, p in enumerate((pos1, pos2, pos3, pos4)):
+            nc.sync.dma_start(pos_sb[d][:], p)
+        for d in range(D):
+            nc.sync.dma_start(out=gates[d][:], in_=gate[d].rearrange("(b p) v -> p b v", p=P))
+
+        x_got = sb([P, 2, S], F32, "x_got")
+        x_group = [sb([P, SLICE, PACK], BF16, f"x_group{s}") for s in range(SLICES)]
+        x_codes = [sb([P, SLICE], U32, f"x_codes{s}") for s in range(SLICES)]
+        x_scales = [sb([P, SLICE], U8, f"x_scales{s}") for s in range(SLICES)]
+        for j in range(2):
+            nc.vector.tensor_copy(x_got[:, j, :], x_raw[j][:].indirect(offs_sb[:]))
+        for s in range(SLICES):
+            nc.scalar.copy(x_group[s][:, :, 0:2], x_got[:, :, s * SLICE : (s + 1) * SLICE].rearrange("p j n -> p n j"))
+
+        def gather_into(s, j):
+            cols = slice(s * SLICE // LANE, (s + 1) * SLICE // LANE)
+            nc.vector.tensor_copy(x_group[s][:, :, j], x_raw[j][:].indirect(offs_sb[:, cols]))
+
+        for s in range(SLICES):
+            gather_into(s, 2)
+
+        w1_group = sb([P, H * PACK], BF16, "w1_group")
+        w1_codes = sb([P, H], U32, "w1_codes")
+        w1_scales = sb([P, H], U8, "w1_scales")
+        w1_out = w1_group[:].rearrange("p (t m j) -> p m j t", t=PACK, j=PACK)
+        w1_in = w1_raw[:].rearrange("p j (m t) -> p m j t", t=PACK)
+        nc.scalar.copy(w1_out[:, 0:64], w1_in[:, 0:64])
+        nc.vector.tensor_copy(w1_out[:, 64:128], w1_in[:, 64:128])
+        nc.vector.quantize_mx(out=w1_codes[:].bitcast(FP8X4), scales=w1_scales[:], in_=w1_group[:])
+
+        def quantize_x(s):
+            nc.vector.quantize_mx(
+                out=x_codes[s][:].bitcast(FP8X4), scales=x_scales[s][:], in_=x_group[s][:].rearrange("p n j -> p (n j)")
+            )
+
+        w2_group = sb([P, N, PACK], BF16, "w2_group")
+        w2_codes = sb([P, N], U32, "w2_codes")
+        w2_scales = sb([P, N], U8, "w2_scales")
+
+        h_group = [sb([P, SLICE, PACK], BF16, f"h_group{s}") for s in range(SLICES)]
+        h_codes = [sb([P, SLICE], U32, f"h_codes{s}") for s in range(SLICES)]
+        h_scales = [sb([P, SLICE], U8, f"h_scales{s}") for s in range(SLICES)]
+
+        def first(s, half, engine):
+            bank = psum.tile([P, PACK, P], F32, name="h_bank", bufs=4)
+            cols = slice(half * P, (half + 1) * P)
+            for t in range(PACK):
+                nc.tensor.matmul_mx(
+                    out=bank[:, t, :],
+                    lhsT=w1_codes[:, t * P : (t + 1) * P].bitcast(FP8X4),
+                    lhsT_scale=w1_scales[:, t * P : (t + 1) * P],
+                    rhs=x_codes[s][:, cols].bitcast(FP8X4),
+                    rhs_scale=x_scales[s][:, cols],
+                    start=True,
+                    stop=True,
+                )
+            dst, src = h_group[s][:, cols, :], bank[:].rearrange("p t n -> p n t")
+            if engine == "scalar":
+                nc.scalar.activation(dst, src, RELU)
+            else:
+                nc.vector.tensor_scalar_max(dst, src, 0.0)
+
+        def quantize_h(s):
+            nc.vector.quantize_mx(
+                out=h_codes[s][:].bitcast(FP8X4), scales=h_scales[s][:], in_=h_group[s][:].rearrange("p n j -> p (n j)")
+            )
+
+        y_ab = [psum.tile([P, 2 * SLICE], F32, name=f"y_ab{b}") for b in range(2)]
+        y_c = [psum.tile([P, SLICE], F32, name=f"y_c{b}") for b in range(2)]
+
+        def second(s, b):
+            dst = y_c[b][:] if s == 2 else y_ab[b][:, s * SLICE : (s + 1) * SLICE]
+            nc.tensor.matmul_mx(
+                out=dst,
+                lhsT=w2_codes[:, b * P : (b + 1) * P].bitcast(FP8X4),
+                lhsT_scale=w2_scales[:, b * P : (b + 1) * P],
+                rhs=h_codes[s][:].bitcast(FP8X4),
+                rhs_scale=h_scales[s][:],
+                start=True,
+                stop=True,
+            )
+
+        gather_into(0, 3)
+        gather_into(1, 3)
+        quantize_x(0)
+        nc.scalar.copy(w2_group[:], w2_raw[:].rearrange("p j n -> p n j"))
+        first(0, 0, "scalar")
+        first(0, 1, "scalar")
+        gather_into(2, 3)
+        quantize_x(1)
+        first(1, 0, "scalar")
+        quantize_x(2)
+        nc.vector.quantize_mx(out=w2_codes[:].bitcast(FP8X4), scales=w2_scales[:], in_=w2_group[:].rearrange("p n j -> p (n j)"))
+        first(1, 1, "vector")
+        quantize_h(0)
+        first(2, 0, "scalar")
+        first(2, 1, "vector")
+        second(0, 0)
+        second(0, 1)
+        quantize_h(1)
+        second(1, 0)
+        second(1, 1)
+        quantize_h(2)
+        second(2, 0)
+        second(2, 1)
+
+        y = [sb([P, S], F32, f"y{b}") for b in range(2)]
+        nc.scalar.copy(y[0][:, 0 : 2 * SLICE], y_ab[0][:])
+        nc.vector.tensor_copy(y[0][:, 2 * SLICE : S], y_c[0][:])
+        nc.scalar.copy(y[1][:, 0 : 2 * SLICE], y_ab[1][:])
+        nc.scalar.copy(y[1][:, 2 * SLICE : S], y_c[1][:])
+
+        turn = [[sb([P, V], F32, f"turn{b}{d}") for d in range(D)] for b in range(2)]
+        sums = [[sb([P, V], F32, f"sum{b}{i}") for i in range(3)] for b in range(2)]
+
+        def fetch(b, d):
+            nc.vector.tensor_tensor(turn[b][d][:], y[b][:].indirect(pos_sb[d][:]), gates[d][:, b, :], MULT)
+
+        def add(dst, a, b, cols=slice(0, V)):
+            nc.vector.tensor_tensor(dst[:, cols], a[:, cols], b[:, cols], ADD)
+
+        for b in range(2):
+            fetch(b, 0)
+            fetch(b, 1)
+            fetch(b, 2)
+            add(sums[b][0], turn[b][0], turn[b][1])
+            fetch(b, 3)
+            halves = [slice(0, V // 2), slice(V // 2, V)]
+            for cols in halves:
+                add(sums[b][1], sums[b][0], turn[b][2], cols)
+            for cols in halves:
+                add(sums[b][2], sums[b][1], turn[b][3], cols)
+                nc.sync.dma_start(out=out[b * P : (b + 1) * P, cols], in_=sums[b][2][:, cols])

@@ -39,24 +39,25 @@ def tile_picked_sub_mlp_relu_sub_e_kernel(tc, xT, w1, w2, gate, offs, pos1, pos2
         gates = [sb([P, N // P, V], F32, f"gate{d}") for d in range(D)]
 
         xv = xT.rearrange("(p j) t -> p j t", j=PACK)
+        nc.sync.dma_start(out=x_raw[0][:], in_=xv[:, 0, :])
         nc.sync.dma_start(offs_sb[:], offs)
-        for j in range(3):
+        for j in range(1, 3):
             nc.sync.dma_start(out=x_raw[j][:], in_=xv[:, j, :])
         nc.sync.dma_start(out=w1_raw[:], in_=w1.rearrange("(p j) c -> p j c", j=PACK))
         nc.sync.dma_start(out=x_raw[3][:], in_=xv[:, 3, :])
         nc.sync.dma_start(out=w2_raw[:], in_=w2.rearrange("(p j) c -> p j c", j=PACK))
         for d, p in enumerate((pos1, pos2, pos3, pos4)):
             nc.sync.dma_start(pos_sb[d][:], p)
-        for d in range(D):
             nc.sync.dma_start(out=gates[d][:], in_=gate[d].rearrange("(b p) v -> p b v", p=P))
 
         x_got = sb([P, 2, S], F32, "x_got")
         x_group = [sb([P, SLICE, PACK], BF16, f"x_group{s}") for s in range(SLICES)]
         x_codes = [sb([P, SLICE], U32, f"x_codes{s}") for s in range(SLICES)]
         x_scales = [sb([P, SLICE], U8, f"x_scales{s}") for s in range(SLICES)]
-        for j in range(2):
-            nc.vector.tensor_copy(x_got[:, j, :], x_raw[j][:].indirect(offs_sb[:]))
+        nc.vector.tensor_copy(x_got[:, 0, :], x_raw[0][:].indirect(offs_sb[:]))
         for s in range(SLICES):
+            cols = slice(s * SLICE // LANE, (s + 1) * SLICE // LANE)
+            nc.vector.tensor_copy(x_got[:, 1, s * SLICE : (s + 1) * SLICE], x_raw[1][:].indirect(offs_sb[:, cols]))
             nc.scalar.copy(x_group[s][:, :, 0:2], x_got[:, :, s * SLICE : (s + 1) * SLICE].rearrange("p j n -> p n j"))
 
         def gather_into(s, j):
@@ -74,6 +75,19 @@ def tile_picked_sub_mlp_relu_sub_e_kernel(tc, xT, w1, w2, gate, offs, pos1, pos2
         nc.scalar.copy(w1_out[:, 0:64], w1_in[:, 0:64])
         nc.vector.tensor_copy(w1_out[:, 64:128], w1_in[:, 64:128])
         nc.vector.quantize_mx(out=w1_codes[:].bitcast(FP8X4), scales=w1_scales[:], in_=w1_group[:])
+
+        y_ab = [psum.tile([P, 2 * SLICE], F32, name=f"y_ab{b}") for b in range(2)]
+        y_c = [psum.tile([P, SLICE], F32, name=f"y_c{b}") for b in range(2)]
+        for b in range(2):
+            nc.tensor.matmul_mx(
+                out=y_ab[b][:],
+                lhsT=w1_codes[:, 0:P].bitcast(FP8X4),
+                lhsT_scale=w1_scales[:, 0:P],
+                rhs=w1_codes[:].bitcast(FP8X4),
+                rhs_scale=w1_scales[:],
+                start=True,
+                stop=True,
+            )
 
         def quantize_x(s):
             nc.vector.quantize_mx(
@@ -112,8 +126,6 @@ def tile_picked_sub_mlp_relu_sub_e_kernel(tc, xT, w1, w2, gate, offs, pos1, pos2
                 out=h_codes[s][:].bitcast(FP8X4), scales=h_scales[s][:], in_=h_group[s][:].rearrange("p n j -> p (n j)")
             )
 
-        y_ab = [psum.tile([P, 2 * SLICE], F32, name=f"y_ab{b}") for b in range(2)]
-        y_c = [psum.tile([P, SLICE], F32, name=f"y_c{b}") for b in range(2)]
 
         def second(s, b):
             dst = y_c[b][:] if s == 2 else y_ab[b][:, s * SLICE : (s + 1) * SLICE]
@@ -130,18 +142,18 @@ def tile_picked_sub_mlp_relu_sub_e_kernel(tc, xT, w1, w2, gate, offs, pos1, pos2
         gather_into(0, 3)
         gather_into(1, 3)
         quantize_x(0)
-        nc.scalar.copy(w2_group[:], w2_raw[:].rearrange("p j n -> p n j"))
         first(0, 0, "scalar")
         first(0, 1, "scalar")
         gather_into(2, 3)
         quantize_x(1)
         first(1, 0, "scalar")
         quantize_x(2)
+        nc.vector.tensor_copy(w2_group[:], w2_raw[:].rearrange("p j n -> p n j"))
         nc.vector.quantize_mx(out=w2_codes[:].bitcast(FP8X4), scales=w2_scales[:], in_=w2_group[:].rearrange("p n j -> p (n j)"))
         first(1, 1, "vector")
         quantize_h(0)
         first(2, 0, "scalar")
-        first(2, 1, "vector")
+        first(2, 1, "scalar")
         second(0, 0)
         second(0, 1)
         quantize_h(1)
@@ -157,24 +169,28 @@ def tile_picked_sub_mlp_relu_sub_e_kernel(tc, xT, w1, w2, gate, offs, pos1, pos2
         nc.scalar.copy(y[1][:, 0 : 2 * SLICE], y_ab[1][:])
         nc.scalar.copy(y[1][:, 2 * SLICE : S], y_c[1][:])
 
-        turn = [[sb([P, V], F32, f"turn{b}{d}") for d in range(D)] for b in range(2)]
-        sums = [[sb([P, V], F32, f"sum{b}{i}") for i in range(3)] for b in range(2)]
+        turn = [sb([P, D, V], F32, f"turn{b}") for b in range(2)]
+        pair = [sb([P, 2, V], F32, f"pair{b}") for b in range(2)]
+        result = [sb([P, V], F32, f"result{b}") for b in range(2)]
 
         def fetch(b, d):
-            nc.vector.tensor_tensor(turn[b][d][:], y[b][:].indirect(pos_sb[d][:]), gates[d][:, b, :], MULT)
+            nc.vector.tensor_tensor(turn[b][:, d, :], y[b][:].indirect(pos_sb[d][:]), gates[d][:, b, :], MULT)
 
-        def add(dst, a, b, cols=slice(0, V)):
-            nc.vector.tensor_tensor(dst[:, cols], a[:, cols], b[:, cols], ADD)
+        def store(b, cols):
+            nc.sync.dma_start(out=out[b * P : (b + 1) * P, cols], in_=result[b][:, cols])
 
-        for b in range(2):
-            fetch(b, 0)
-            fetch(b, 1)
-            fetch(b, 2)
-            add(sums[b][0], turn[b][0], turn[b][1])
-            fetch(b, 3)
-            halves = [slice(0, V // 2), slice(V // 2, V)]
-            for cols in halves:
-                add(sums[b][1], sums[b][0], turn[b][2], cols)
-            for cols in halves:
-                add(sums[b][2], sums[b][1], turn[b][3], cols)
-                nc.sync.dma_start(out=out[b * P : (b + 1) * P, cols], in_=sums[b][2][:, cols])
+        for d in range(D):
+            fetch(0, d)
+        fetch(1, 0)
+        nc.vector.tensor_tensor(pair[0][:], turn[0][:, 0:2, :], turn[0][:, 2:4, :], ADD)
+        fetch(1, 1)
+        nc.vector.tensor_tensor(result[0][:], pair[0][:, 0, :], pair[0][:, 1, :], ADD)
+        store(0, slice(0, V))
+        fetch(1, 2)
+        nc.vector.tensor_tensor(pair[1][:, 0, :], turn[1][:, 0, :], turn[1][:, 1, :], ADD)
+        fetch(1, 3)
+        halves = [slice(0, V // 2), slice(V // 2, V)]
+        nc.vector.tensor_tensor(pair[1][:, 1, :], pair[1][:, 0, :], turn[1][:, 2, :], ADD)
+        for cols in halves:
+            nc.vector.tensor_tensor(result[1][:, cols], pair[1][:, 1, cols], turn[1][:, 3, cols], ADD)
+            store(1, cols)

@@ -76,11 +76,11 @@ def tile_picked_sub_mlp_relu_sub_e_kernel(tc, xT, w1, w2, gate, offs, pos1, pos2
         nc.vector.tensor_copy(w1_out[:, 64:128], w1_in[:, 64:128])
         nc.vector.quantize_mx(out=w1_codes[:].bitcast(FP8X4), scales=w1_scales[:], in_=w1_group[:])
 
-        y_ab = [psum.tile([P, 2 * SLICE], F32, name=f"y_ab{b}") for b in range(2)]
-        y_c = [psum.tile([P, SLICE], F32, name=f"y_c{b}") for b in range(2)]
+        y_psum = [psum.tile([P, SLICE], F32, name=f"y_psum{s}") for s in range(SLICES)]
         for b in range(2):
+            warm = psum.tile([P, H], F32, name="h_bank", bufs=5)
             nc.tensor.matmul_mx(
-                out=y_ab[b][:],
+                out=warm[:],
                 lhsT=w1_codes[:, 0:P].bitcast(FP8X4),
                 lhsT_scale=w1_scales[:, 0:P],
                 rhs=w1_codes[:].bitcast(FP8X4),
@@ -94,16 +94,24 @@ def tile_picked_sub_mlp_relu_sub_e_kernel(tc, xT, w1, w2, gate, offs, pos1, pos2
                 out=x_codes[s][:].bitcast(FP8X4), scales=x_scales[s][:], in_=x_group[s][:].rearrange("p n j -> p (n j)")
             )
 
-        w2_group = sb([P, N, PACK], BF16, "w2_group")
-        w2_codes = sb([P, N], U32, "w2_codes")
-        w2_scales = sb([P, N], U8, "w2_scales")
+        w2_group = [sb([P, P, PACK], BF16, f"w2_group{b}") for b in range(2)]
+        w2_codes = [sb([P, P], U32, f"w2_codes{b}") for b in range(2)]
+        w2_scales = [sb([P, P], U8, f"w2_scales{b}") for b in range(2)]
+
+        def interleave_w2(b):
+            nc.scalar.copy(w2_group[b][:], w2_raw[:, :, b * P : (b + 1) * P].rearrange("p j n -> p n j"))
+
+        def quantize_w2(b):
+            nc.vector.quantize_mx(
+                out=w2_codes[b][:].bitcast(FP8X4), scales=w2_scales[b][:], in_=w2_group[b][:].rearrange("p n j -> p (n j)")
+            )
 
         h_group = [sb([P, SLICE, PACK], BF16, f"h_group{s}") for s in range(SLICES)]
         h_codes = [sb([P, SLICE], U32, f"h_codes{s}") for s in range(SLICES)]
         h_scales = [sb([P, SLICE], U8, f"h_scales{s}") for s in range(SLICES)]
 
         def first(s, half, engine):
-            bank = psum.tile([P, PACK, P], F32, name="h_bank", bufs=4)
+            bank = psum.tile([P, PACK, P], F32, name="h_bank", bufs=5)
             cols = slice(half * P, (half + 1) * P)
             for t in range(PACK):
                 nc.tensor.matmul_mx(
@@ -128,11 +136,11 @@ def tile_picked_sub_mlp_relu_sub_e_kernel(tc, xT, w1, w2, gate, offs, pos1, pos2
 
 
         def second(s, b):
-            dst = y_c[b][:] if s == 2 else y_ab[b][:, s * SLICE : (s + 1) * SLICE]
+            dst = y_psum[s][:] if b == 0 else y1_psum[s // 2][:, s % 2 * SLICE : (s % 2 + 1) * SLICE]
             nc.tensor.matmul_mx(
                 out=dst,
-                lhsT=w2_codes[:, b * P : (b + 1) * P].bitcast(FP8X4),
-                lhsT_scale=w2_scales[:, b * P : (b + 1) * P],
+                lhsT=w2_codes[b][:].bitcast(FP8X4),
+                lhsT_scale=w2_scales[b][:],
                 rhs=h_codes[s][:].bitcast(FP8X4),
                 rhs_scale=h_scales[s][:],
                 start=True,
@@ -142,33 +150,33 @@ def tile_picked_sub_mlp_relu_sub_e_kernel(tc, xT, w1, w2, gate, offs, pos1, pos2
         gather_into(0, 3)
         gather_into(1, 3)
         quantize_x(0)
+        interleave_w2(0)
         first(0, 0, "scalar")
         first(0, 1, "scalar")
         gather_into(2, 3)
         quantize_x(1)
         first(1, 0, "scalar")
         quantize_x(2)
-        nc.vector.tensor_copy(w2_group[:], w2_raw[:].rearrange("p j n -> p n j"))
-        nc.vector.quantize_mx(out=w2_codes[:].bitcast(FP8X4), scales=w2_scales[:], in_=w2_group[:].rearrange("p n j -> p (n j)"))
+        quantize_w2(0)
         first(1, 1, "vector")
         quantize_h(0)
         first(2, 0, "scalar")
-        first(2, 1, "scalar")
+        interleave_w2(1)
+        first(2, 1, "vector")
+        y = [sb([P, S], F32, f"y{b}") for b in range(2)]
+
+        def leave(engine, s):
+            engine(y[0][:, s * SLICE : (s + 1) * SLICE], y_psum[s][:])
+
         second(0, 0)
-        second(0, 1)
+        leave(nc.scalar.copy, 0)
         quantize_h(1)
         second(1, 0)
-        second(1, 1)
+        leave(nc.scalar.copy, 1)
         quantize_h(2)
+        quantize_w2(1)
         second(2, 0)
-        second(2, 1)
-
-        y = [sb([P, S], F32, f"y{b}") for b in range(2)]
-        nc.scalar.copy(y[0][:, 0 : 2 * SLICE], y_ab[0][:])
-        nc.vector.tensor_copy(y[0][:, 2 * SLICE : S], y_c[0][:])
-        nc.scalar.copy(y[1][:, 0 : 2 * SLICE], y_ab[1][:])
-        nc.scalar.copy(y[1][:, 2 * SLICE : S], y_c[1][:])
-
+        leave(nc.vector.tensor_copy, 2)
         turn = [sb([P, D, V], F32, f"turn{b}") for b in range(2)]
         pair = [sb([P, 2, V], F32, f"pair{b}") for b in range(2)]
         result = [sb([P, V], F32, f"result{b}") for b in range(2)]
@@ -179,7 +187,13 @@ def tile_picked_sub_mlp_relu_sub_e_kernel(tc, xT, w1, w2, gate, offs, pos1, pos2
         def store(b, cols):
             nc.sync.dma_start(out=out[b * P : (b + 1) * P, cols], in_=result[b][:, cols])
 
-        for d in range(D):
+        fetch(0, 0)
+        y1_psum = [psum.tile([P, 2 * SLICE], F32, name="h_bank", bufs=5) for i in range(2)]
+        for s in range(SLICES):
+            second(s, 1)
+        nc.scalar.copy(y[1][:, 0 : 2 * SLICE], y1_psum[0][:])
+        nc.scalar.copy(y[1][:, 2 * SLICE : S], y1_psum[1][:, 0:SLICE])
+        for d in range(1, D):
             fetch(0, d)
         fetch(1, 0)
         nc.vector.tensor_tensor(pair[0][:], turn[0][:, 0:2, :], turn[0][:, 2:4, :], ADD)

@@ -181,8 +181,9 @@ def tile_picked_sub_mlp_relu_sub_e_kernel(tc, xT, w1, w2, gate, offs, pos1, pos2
         pair = [sb([P, 2, V], F32, f"pair{b}") for b in range(2)]
         result = [sb([P, V], F32, f"result{b}") for b in range(2)]
 
-        def fetch(b, d):
-            nc.vector.tensor_tensor(turn[b][:, d, :], y[b][:].indirect(pos_sb[d][:]), gates[d][:, b, :], MULT)
+        def fetch(b, d, cols=slice(0, V)):
+            places = pos_sb[d][:, cols.start // LANE : cols.stop // LANE]
+            nc.vector.tensor_tensor(turn[b][:, d, cols], y[b][:].indirect(places), gates[d][:, b, cols], MULT)
 
         def store(b, cols):
             nc.sync.dma_start(out=out[b * P : (b + 1) * P, cols], in_=result[b][:, cols])
@@ -196,15 +197,16 @@ def tile_picked_sub_mlp_relu_sub_e_kernel(tc, xT, w1, w2, gate, offs, pos1, pos2
         for d in range(1, D):
             fetch(0, d)
         fetch(1, 0)
-        nc.vector.tensor_tensor(pair[0][:], turn[0][:, 0:2, :], turn[0][:, 2:4, :], ADD)
         fetch(1, 1)
+        nc.vector.tensor_tensor(pair[0][:], turn[0][:, 0:2, :], turn[0][:, 2:4, :], ADD)
+        nc.vector.tensor_tensor(pair[1][:, 0, :], turn[1][:, 0, :], turn[1][:, 1, :], ADD)
+        fetch(1, 2)
         nc.vector.tensor_tensor(result[0][:], pair[0][:, 0, :], pair[0][:, 1, :], ADD)
         store(0, slice(0, V))
-        fetch(1, 2)
-        nc.vector.tensor_tensor(pair[1][:, 0, :], turn[1][:, 0, :], turn[1][:, 1, :], ADD)
-        fetch(1, 3)
-        halves = [slice(0, V // 2), slice(V // 2, V)]
         nc.vector.tensor_tensor(pair[1][:, 1, :], pair[1][:, 0, :], turn[1][:, 2, :], ADD)
-        for cols in halves:
+        ends = [slice(0, 256), slice(256, V)]
+        for cols in ends:
+            fetch(1, 3, cols)
+        for cols in ends:
             nc.vector.tensor_tensor(result[1][:, cols], pair[1][:, 1, cols], turn[1][:, 3, cols], ADD)
             store(1, cols)

from contextlib import ExitStack

import concourse.mybir as mybir

K, T, D, S, V, H, N = 512, 2048, 4, 768, 384, 512, 256
FLOPS = 2 * S * (K * H + H * N)

F32 = mybir.dt.float32
BF16 = mybir.dt.bfloat16
U32 = mybir.dt.uint32
U16 = mybir.dt.uint16
U8 = mybir.dt.uint8
FP8X4 = mybir.dt.float8_e4m3fn_x4
ADD, MULT = mybir.AluOpType.add, mybir.AluOpType.mult
RELU = mybir.ActivationFunctionType.Relu

P = 128
PACK = 4
SLICE = 256
SLICES = S // SLICE
LANE = 16


def tile_picked_sub_mlp_relu_sub_e_kernel(tc, xT, w1, w2, gate, offs, pos1, pos2, pos3, pos4, out):
    nc = tc.nc
    with ExitStack() as ctx:
        keep = ctx.enter_context(tc.tile_pool(name="keep", bufs=1))
        psum = ctx.enter_context(tc.psum_pool(name="psum", bufs=1))

        def sb(shape, dtype, name):
            return keep.tile(shape, dtype, name=name, align_bytes=64)

        offs_sb = keep.tile([P, S // LANE], U16, name="offs_sb")
        pos_sb = [keep.tile([P, V // LANE], U16, name=f"pos_sb{d}") for d in range(D)]

        x_raw = [sb([P, T], F32, f"x_raw{j}") for j in range(PACK)]
        w1_raw = sb([P, PACK, H], F32, "w1_raw")
        w2_raw = sb([P, PACK, N], F32, "w2_raw")
        gates = [sb([P, N // P, V], F32, f"gate{d}") for d in range(D)]

        xv = xT.rearrange("(p j) t -> p j t", j=PACK)
        nc.sync.dma_start(out=x_raw[0][:], in_=xv[:, 0, :])
        nc.sync.dma_start(offs_sb[:], offs)
        for j in range(1, 3):
            nc.sync.dma_start(out=x_raw[j][:], in_=xv[:, j, :])
        nc.sync.dma_start(out=w1_raw[:], in_=w1.rearrange("(p j) c -> p j c", j=PACK))
        nc.sync.dma_start(out=x_raw[3][:], in_=xv[:, 3, :])
        nc.sync.dma_start(out=w2_raw[:], in_=w2.rearrange("(p j) c -> p j c", j=PACK))
        for d, p in enumerate((pos1, pos2, pos3, pos4)):
            nc.sync.dma_start(pos_sb[d][:], p)
            nc.sync.dma_start(out=gates[d][:], in_=gate[d].rearrange("(b p) v -> p b v", p=P))

        x_got = sb([P, 2, S], F32, "x_got")
        x_group = [sb([P, SLICE, PACK], BF16, f"x_group{s}") for s in range(SLICES)]
        x_codes = [sb([P, SLICE], U32, f"x_codes{s}") for s in range(SLICES)]
        x_scales = [sb([P, SLICE], U8, f"x_scales{s}") for s in range(SLICES)]
        nc.vector.tensor_copy(x_got[:, 0, :], x_raw[0][:].indirect(offs_sb[:]))
        for s in range(SLICES):
            cols = slice(s * SLICE // LANE, (s + 1) * SLICE // LANE)
            nc.vector.tensor_copy(x_got[:, 1, s * SLICE : (s + 1) * SLICE], x_raw[1][:].indirect(offs_sb[:, cols]))
            nc.scalar.copy(x_group[s][:, :, 0:2], x_got[:, :, s * SLICE : (s + 1) * SLICE].rearrange("p j n -> p n j"))

        def gather_into(s, j):
            cols = slice(s * SLICE // LANE, (s + 1) * SLICE // LANE)
            nc.vector.tensor_copy(x_group[s][:, :, j], x_raw[j][:].indirect(offs_sb[:, cols]))

        for s in range(SLICES):
            gather_into(s, 2)

        w1_group = sb([P, H * PACK], BF16, "w1_group")
        w1_codes = sb([P, H], U32, "w1_codes")
        w1_scales = sb([P, H], U8, "w1_scales")
        w1_out = w1_group[:].rearrange("p (t m j) -> p m j t", t=PACK, j=PACK)
        w1_in = w1_raw[:].rearrange("p j (m t) -> p m j t", t=PACK)
        nc.scalar.copy(w1_out[:, 0:64], w1_in[:, 0:64])
        nc.vector.tensor_copy(w1_out[:, 64:128], w1_in[:, 64:128])
        nc.vector.quantize_mx(out=w1_codes[:].bitcast(FP8X4), scales=w1_scales[:], in_=w1_group[:])

        y_psum = [psum.tile([P, SLICE], F32, name=f"y_psum{s}") for s in range(SLICES)]
        for b in range(2):
            warm = psum.tile([P, H], F32, name="h_bank", bufs=5)
            nc.tensor.matmul_mx(
                out=warm[:],
                lhsT=w1_codes[:, 0:P].bitcast(FP8X4),
                lhsT_scale=w1_scales[:, 0:P],
                rhs=w1_codes[:].bitcast(FP8X4),
                rhs_scale=w1_scales[:],
                start=True,
                stop=True,
            )

        def quantize_x(s):
            nc.vector.quantize_mx(
                out=x_codes[s][:].bitcast(FP8X4), scales=x_scales[s][:], in_=x_group[s][:].rearrange("p n j -> p (n j)")
            )

        w2_group = [sb([P, P, PACK], BF16, f"w2_group{b}") for b in range(2)]
        w2_codes = [sb([P, P], U32, f"w2_codes{b}") for b in range(2)]
        w2_scales = [sb([P, P], U8, f"w2_scales{b}") for b in range(2)]

        def interleave_w2(b):
            nc.scalar.copy(w2_group[b][:], w2_raw[:, :, b * P : (b + 1) * P].rearrange("p j n -> p n j"))

        def quantize_w2(b):
            nc.vector.quantize_mx(
                out=w2_codes[b][:].bitcast(FP8X4), scales=w2_scales[b][:], in_=w2_group[b][:].rearrange("p n j -> p (n j)")
            )

        h_group = [sb([P, SLICE, PACK], BF16, f"h_group{s}") for s in range(SLICES)]
        h_codes = [sb([P, SLICE], U32, f"h_codes{s}") for s in range(SLICES)]
        h_scales = [sb([P, SLICE], U8, f"h_scales{s}") for s in range(SLICES)]

        def first(s, half, engine):
            bank = psum.tile([P, PACK, P], F32, name="h_bank", bufs=5)
            cols = slice(half * P, (half + 1) * P)
            for t in range(PACK):
                nc.tensor.matmul_mx(
                    out=bank[:, t, :],
                    lhsT=w1_codes[:, t * P : (t + 1) * P].bitcast(FP8X4),
                    lhsT_scale=w1_scales[:, t * P : (t + 1) * P],
                    rhs=x_codes[s][:, cols].bitcast(FP8X4),
                    rhs_scale=x_scales[s][:, cols],
                    start=True,
                    stop=True,
                )
            dst, src = h_group[s][:, cols, :], bank[:].rearrange("p t n -> p n t")
            if engine == "scalar":
                nc.scalar.activation(dst, src, RELU)
            else:
                nc.vector.tensor_scalar_max(dst, src, 0.0)

        def quantize_h(s):
            nc.vector.quantize_mx(
                out=h_codes[s][:].bitcast(FP8X4), scales=h_scales[s][:], in_=h_group[s][:].rearrange("p n j -> p (n j)")
            )


        def second(s, b):
            dst = y_psum[s][:] if b == 0 else y1_psum[s // 2][:, s % 2 * SLICE : (s % 2 + 1) * SLICE]
            nc.tensor.matmul_mx(
                out=dst,
                lhsT=w2_codes[b][:].bitcast(FP8X4),
                lhsT_scale=w2_scales[b][:],
                rhs=h_codes[s][:].bitcast(FP8X4),
                rhs_scale=h_scales[s][:],
                start=True,
                stop=True,
            )

        gather_into(0, 3)
        gather_into(1, 3)
        quantize_x(0)
        interleave_w2(0)
        first(0, 0, "scalar")
        first(0, 1, "scalar")
        gather_into(2, 3)
        quantize_x(1)
        first(1, 0, "scalar")
        quantize_x(2)
        quantize_w2(0)
        first(1, 1, "vector")
        quantize_h(0)
        first(2, 0, "scalar")
        interleave_w2(1)
        first(2, 1, "vector")
        y = [sb([P, S], F32, f"y{b}") for b in range(2)]

        def leave(engine, s):
            engine(y[0][:, s * SLICE : (s + 1) * SLICE], y_psum[s][:])

        second(0, 0)
        leave(nc.scalar.copy, 0)
        quantize_h(1)
        second(1, 0)
        leave(nc.scalar.copy, 1)
        quantize_h(2)
        quantize_w2(1)
        second(2, 0)
        leave(nc.vector.tensor_copy, 2)
        turn = [sb([P, D, V], F32, f"turn{b}") for b in range(2)]
        pair = [sb([P, 2, V], F32, f"pair{b}") for b in range(2)]
        result = [sb([P, V], F32, f"result{b}") for b in range(2)]

        def fetch(b, d, cols=slice(0, V)):
            places = pos_sb[d][:, cols.start // LANE : cols.stop // LANE]
            nc.vector.tensor_tensor(turn[b][:, d, cols], y[b][:].indirect(places), gates[d][:, b, cols], MULT)

        def store(b, cols):
            nc.sync.dma_start(out=out[b * P : (b + 1) * P, cols], in_=result[b][:, cols])

        fetch(0, 0)
        y1_psum = [psum.tile([P, 2 * SLICE], F32, name="h_bank", bufs=5) for i in range(2)]
        for s in range(SLICES):
            second(s, 1)
        nc.scalar.copy(y[1][:, 0 : 2 * SLICE], y1_psum[0][:])
        nc.scalar.copy(y[1][:, 2 * SLICE : S], y1_psum[1][:, 0:SLICE])
        for d in range(1, D):
            fetch(0, d)
        fetch(1, 0)
        fetch(1, 1)
        nc.vector.tensor_tensor(pair[0][:], turn[0][:, 0:2, :], turn[0][:, 2:4, :], ADD)
        nc.vector.tensor_tensor(pair[1][:, 0, :], turn[1][:, 0, :], turn[1][:, 1, :], ADD)
        fetch(1, 2)
        nc.vector.tensor_tensor(result[0][:], pair[0][:, 0, :], pair[0][:, 1, :], ADD)
        store(0, slice(0, V))
        nc.vector.tensor_tensor(pair[1][:, 1, :], pair[1][:, 0, :], turn[1][:, 2, :], ADD)
        ends = [slice(0, 256), slice(256, V)]
        for cols in ends:
            fetch(1, 3, cols)
        for cols in ends:
            nc.vector.tensor_tensor(result[1][:, cols], pair[1][:, 1, cols], turn[1][:, 3, cols], ADD)
            store(1, cols)
